import numpy as np
import ml_dtypes


def mxq(x, axis, fmt="e4m3"):
    dtype, down = {"e4m3": (ml_dtypes.float8_e4m3fn, 7), "e5m2": (ml_dtypes.float8_e5m2, 14)}[fmt]
    v = np.moveaxis(np.asarray(x, np.float32).astype(ml_dtypes.bfloat16).astype(np.float64), axis, -1)
    blocks = v.reshape(v.shape[:-1] + (-1, 32))
    amax = np.abs(blocks).max(-1, keepdims=True)
    byte = np.maximum(np.where(amax > 0, np.frexp(amax)[1] - 1 + 127, 0) - down, 1)
    scale = np.exp2(byte - 127.0)
    codes = (blocks / scale).astype(np.float32).astype(dtype).astype(np.float64)
    return np.moveaxis((codes * scale).reshape(v.shape), -1, axis)


WIDE = False


def mx_kscale(k):
    if not WIDE:
        return np.ones(k)
    levels = np.array([10, -10, 5, -5, 0])
    if k % 512:
        return np.exp2(np.random.permutation(np.resize(levels, k // 32))).repeat(32)
    a = np.empty((k // 512, 16))
    for p in range(k // 512):
        a[p, :8] = np.random.permutation(np.resize(levels, 8))
        for g in range(8):
            far = levels[np.abs(levels - a[p, g]) >= 10]
            a[p, g + 8] = far[np.random.randint(len(far))]
    return np.exp2(a.ravel()).repeat(32)


def f64(x):
    return np.asarray(x).astype(np.float64)


def striped(idx):
    return np.tile(idx.reshape(-1, 16).T, (8, 1)).astype(np.uint16)


def unstriped(offs):
    return offs[:16].T.reshape(-1).astype(np.int64)


def silu(v):
    return v / (1.0 + np.exp(-np.maximum(v, -700.0)))


K, T, E, C, N = 1536, 1024, 2, 256, 256


def by_expert(wq, xq):
    return np.concatenate([wq[e].T @ xq[:, e * C:(e + 1) * C] for e in range(E)], axis=1)


def setup_inputs():
    n = np.random.standard_normal
    s = mx_kscale(K)[:, None]
    return {
        "xT": (n((K, T)) * s).astype(np.float32),
        "w": (n((E, K, N)) / np.sqrt(K) / s[None]).astype(np.float32),
        "b": (0.3 * n((N, E))).astype(np.float32),
        "gate": np.tile(np.random.uniform(0.2, 1.0, E * C), (N, 1)).astype(np.float32),
        "offs": striped(np.random.permutation(T)[:E * C]),
    }


def reference(xT, w, b, gate, offs):
    idx = unstriped(offs)
    xq = mxq(f64(xT)[:, idx], 0, "e4m3")
    y = by_expert(mxq(f64(w), 1, "e4m3"), xq)
    y = silu(y + np.repeat(f64(b), C, axis=1))
    out = np.zeros((N, T))
    out[:, idx] = f64(gate) * y
    return out

@@ -1,0 +1,184 @@
+from contextlib import ExitStack
+
+import concourse.mybir as mybir
+
+K, T, E, C, N = 1536, 1024, 2, 256, 256
+FLOPS = 2 * K * N * E * C
+
+F32 = mybir.dt.float32
+BF16 = mybir.dt.bfloat16
+U32 = mybir.dt.uint32
+U16 = mybir.dt.uint16
+U8 = mybir.dt.uint8
+FP8X4 = mybir.dt.float8_e4m3fn_x4
+SILU = mybir.ActivationFunctionType.Silu
+MULT = mybir.AluOpType.mult
+
+P = 128
+PACK = 4
+PASSES = K // (P * PACK)
+BLOCKS = N // P
+SLOTS = E * C
+HALF = T // 2
+X_SPLIT = 320
+W_SPLIT = 256
+LAST_SPLIT = 128
+
+
+def tile_routed_moe_kernel(tc, xT, w, b, gate, offs, out):
+    nc = tc.nc
+    x_rows = xT.rearrange("(g p t) n -> g p t n", p=P, t=PACK)
+    w_rows = w.rearrange("e (g p t) n -> e g p t n", p=P, t=PACK)
+
+    with ExitStack() as ctx:
+        keep = ctx.enter_context(tc.tile_pool(name="keep", bufs=1))
+        psum = ctx.enter_context(tc.psum_pool(name="psum", bufs=1))
+
+        offsets = keep.tile([P, SLOTS // 16], U16, name="offsets")
+        bias = keep.tile([P, BLOCKS, E], F32, name="bias")
+        gates = keep.tile([P, SLOTS], F32, name="gates")
+        x_raw, w_raw = {}, {}
+
+        def load_x(g, h):
+            x_raw[g, h] = keep.tile([P, PACK, HALF], F32, name=f"x_raw{g}{h}", align_bytes=64)
+            nc.sync.dma_start(out=x_raw[g, h][:], in_=x_rows[g, :, :, h * HALF : (h + 1) * HALF])
+
+        def load_w(e, g):
+            w_raw[e, g] = keep.tile([P, PACK, N], F32, name=f"w_raw{e}{g}", align_bytes=64)
+            nc.sync.dma_start(out=w_raw[e, g][:], in_=w_rows[e, g])
+
+        load_x(0, 0)
+        nc.sync.dma_start(offsets[:], offs)
+        nc.scalar.dma_start(out=bias[:], in_=b.rearrange("(m p) e -> p m e", p=P))
+        for g, h in ((0, 1), (1, 0), (1, 1), (2, 0), (2, 1)):
+            load_x(g, h)
+        for g in range(PASSES):
+            load_w(0, g)
+        nc.sync.dma_start(out=gates[:], in_=gate[0:P, :])
+        for g in range(PASSES):
+            load_w(1, g)
+
+        warm = keep.tile([P, 1], F32, name="warm")
+        nc.vector.memset(warm[:], 0.0)
+        nc.scalar.activation(warm[:], warm[:], SILU)
+
+        x_scales = keep.tile([P, T], U8, name="x_scales", align_bytes=64)
+        nc.gpsimd.memset(x_scales[:], 0)
+        windows = []
+        for m in range(BLOCKS):
+            windows.append(keep.tile([P, T], F32, name=f"window{m}"))
+            nc.gpsimd.memset(windows[m][:], 0.0)
+
+        x_codes = [keep.tile([P, T], U32, name=f"x_codes{g}", align_bytes=64) for g in range(PASSES)]
+        slot_codes = [keep.tile([P, SLOTS], U32, name=f"slot_codes{g}", align_bytes=64) for g in range(PASSES)]
+        slot_scales = keep.tile([P, SLOTS], U8, name="slot_scales", align_bytes=64)
+        x_mx, w_mx, w_codes, w_scales = {}, {}, {}, {}
+
+        def interleave(copy, dst, raw, a, z):
+            copy(
+                dst[:, a:z, :].rearrange("p (c i) t -> p c t i", i=4),
+                raw[:, :, a:z].rearrange("p t (c i) -> p c t i", i=4),
+            )
+
+        def cast_x(g, h):
+            x_mx[g, h] = keep.tile([P, HALF, PACK], BF16, name=f"x_mx{g}{h}", align_bytes=64)
+            interleave(nc.scalar.copy, x_mx[g, h], x_raw[g, h], 0, X_SPLIT)
+            interleave(nc.vector.tensor_copy, x_mx[g, h], x_raw[g, h], X_SPLIT, HALF)
+
+        def cast_w(e, g):
+            w_mx[e, g] = keep.tile([P, N, PACK], BF16, name=f"w_mx{e}{g}", align_bytes=64)
+            split = LAST_SPLIT if (e, g) == (E - 1, PASSES - 1) else W_SPLIT
+            interleave(nc.scalar.copy, w_mx[e, g], w_raw[e, g], 0, split)
+            if split < N:
+                interleave(nc.vector.tensor_copy, w_mx[e, g], w_raw[e, g], split, N)
+
+        def quantize_x(g, h):
+            cols = slice(h * HALF, (h + 1) * HALF)
+            nc.vector.quantize_mx(
+                out=x_codes[g][:, cols].bitcast(FP8X4),
+                scales=x_scales[4 * g : P, cols],
+                in_=x_mx[g, h][:].rearrange("p n t -> p (n t)"),
+            )
+
+        def quantize_w(e, g):
+            w_codes[e, g] = keep.tile([P, N], U32, name=f"w_codes{e}{g}", align_bytes=64)
+            w_scales[e, g] = keep.tile([P, N], U8, name=f"w_scales{e}{g}", align_bytes=64)
+            nc.vector.quantize_mx(
+                out=w_codes[e, g][:].bitcast(FP8X4),
+                scales=w_scales[e, g][:],
+                in_=w_mx[e, g][:].rearrange("p n t -> p (n t)"),
+            )
+
+        def gather_codes(g):
+            nc.vector.tensor_copy(slot_codes[g][:], x_codes[g][:].indirect(offsets[:]))
+
+        acc = {}
+
+        def multiply(e, g):
+            slots = slice(e * C, (e + 1) * C)
+            for m in range(BLOCKS):
+                if g == 0:
+                    acc[e, m] = psum.tile([P, C], F32, name=f"acc{e}{m}")
+                feats = slice(m * P, (m + 1) * P)
+                nc.tensor.matmul_mx(
+                    out=acc[e, m][:],
+                    lhsT=w_codes[e, g][:, feats].bitcast(FP8X4),
+                    lhsT_scale=w_scales[e, g][:, feats],
+                    rhs=slot_codes[g][:, slots].bitcast(FP8X4),
+                    rhs_scale=slot_scales[4 * g : P, slots],
+                    start=(g == 0),
+                    stop=(g == PASSES - 1),
+                )
+
+        def finish(e):
+            slots = slice(e * C, (e + 1) * C)
+            y = []
+            for m in range(BLOCKS):
+                y.append(keep.tile([P, C], F32, name=f"y{e}{m}"))
+                nc.scalar.activation(y[m][:], acc[e, m][:], SILU, bias=bias[:, m, e : e + 1])
+            for m in range(BLOCKS):
+                nc.vector.tensor_tensor(
+                    windows[m][:].indirect(offsets[:, e * C // 16 : (e + 1) * C // 16]),
+                    y[m][:],
+                    gates[:, slots],
+                    MULT,
+                )
+                if e == E - 1:
+                    nc.sync.dma_start(out=out[m * P : (m + 1) * P, :], in_=windows[m][:])
+
+        cast_x(0, 0)
+        cast_x(0, 1)
+        quantize_x(0, 0)
+        cast_x(1, 0)
+        quantize_x(0, 1)
+        cast_x(1, 1)
+        quantize_x(1, 0)
+        gather_codes(0)
+        cast_x(2, 0)
+        quantize_x(1, 1)
+        cast_x(2, 1)
+        quantize_x(2, 0)
+        gather_codes(1)
+        cast_w(0, 0)
+        quantize_x(2, 1)
+        cast_w(0, 1)
+        quantize_w(0, 0)
+        nc.vector.tensor_copy(slot_scales[:], x_scales[:].indirect(offsets[:]))
+        multiply(0, 0)
+        cast_w(0, 2)
+        quantize_w(0, 1)
+        gather_codes(2)
+        multiply(0, 1)
+        cast_w(1, 0)
+        quantize_w(0, 2)
+        multiply(0, 2)
+        cast_w(1, 1)
+        quantize_w(1, 0)
+        multiply(1, 0)
+        finish(0)
+        quantize_w(1, 1)
+        multiply(1, 1)
+        cast_w(1, 2)
+        quantize_w(1, 2)
+        multiply(1, 2)
+        finish(1)

@@ -19,10 +19,7 @@ PACK = 4
 PASSES = K // (P * PACK)
 BLOCKS = N // P
 SLOTS = E * C
-HALF = T // 2
-X_SPLIT = 320
-W_SPLIT = 256
-LAST_SPLIT = 128
+PIECE = 512
 
 
 def tile_routed_moe_kernel(tc, xT, w, b, gate, offs, out):
@@ -39,24 +36,30 @@ def tile_routed_moe_kernel(tc, xT, w, b, gate, offs, out):
         gates = keep.tile([P, SLOTS], F32, name="gates")
         x_raw, w_raw = {}, {}
 
-        def load_x(g, h):
-            x_raw[g, h] = keep.tile([P, PACK, HALF], F32, name=f"x_raw{g}{h}", align_bytes=64)
-            nc.sync.dma_start(out=x_raw[g, h][:], in_=x_rows[g, :, :, h * HALF : (h + 1) * HALF])
+        def load_x(g, a, z):
+            raw = keep.tile([P, PACK, z - a], F32, name=f"x_raw{g}_{a}", align_bytes=64)
+            nc.sync.dma_start(out=raw[:], in_=x_rows[g, :, :, a:z])
+            for token in range(a, z, PIECE):
+                x_raw[g, token] = raw[:, :, token - a : min(z, token + PIECE) - a]
 
         def load_w(e, g):
-            w_raw[e, g] = keep.tile([P, PACK, N], F32, name=f"w_raw{e}{g}", align_bytes=64)
-            nc.sync.dma_start(out=w_raw[e, g][:], in_=w_rows[e, g])
+            raw = keep.tile([P, PACK, N], F32, name=f"w_raw{e}{g}", align_bytes=64)
+            nc.sync.dma_start(out=raw[:], in_=w_rows[e, g])
+            w_raw[e, g] = raw[:]
 
-        load_x(0, 0)
+        load_x(0, 0, 1024)
         nc.sync.dma_start(offsets[:], offs)
         nc.scalar.dma_start(out=bias[:], in_=b.rearrange("(m p) e -> p m e", p=P))
-        for g, h in ((0, 1), (1, 0), (1, 1), (2, 0), (2, 1)):
-            load_x(g, h)
-        for g in range(PASSES):
-            load_w(0, g)
+        load_x(1, 0, 1024)
+        load_x(2, 0, 512)
+        load_x(2, 512, 1024)
         nc.sync.dma_start(out=gates[:], in_=gate[0:P, :])
-        for g in range(PASSES):
-            load_w(1, g)
+        load_w(0, 0)
+        load_w(0, 1)
+        load_w(0, 2)
+        load_w(1, 0)
+        load_w(1, 1)
+        load_w(1, 2)
 
         warm = keep.tile([P, 1], F32, name="warm")
         nc.vector.memset(warm[:], 0.0)
@@ -80,24 +83,25 @@ def tile_routed_moe_kernel(tc, xT, w, b, gate, offs, out):
                 raw[:, :, a:z].rearrange("p t (c i) -> p c t i", i=4),
             )
 
-        def cast_x(g, h):
-            x_mx[g, h] = keep.tile([P, HALF, PACK], BF16, name=f"x_mx{g}{h}", align_bytes=64)
-            interleave(nc.scalar.copy, x_mx[g, h], x_raw[g, h], 0, X_SPLIT)
-            interleave(nc.vector.tensor_copy, x_mx[g, h], x_raw[g, h], X_SPLIT, HALF)
+        def cast_x(g, a, z, s):
+            x_mx[g, a] = keep.tile([P, z - a, PACK], BF16, name=f"x_mx{g}_{a}", align_bytes=64)
+            if s:
+                interleave(nc.scalar.copy, x_mx[g, a], x_raw[g, a], 0, s)
+            if s < z - a:
+                interleave(nc.vector.tensor_copy, x_mx[g, a], x_raw[g, a], s, z - a)
 
-        def cast_w(e, g):
+        def cast_w(e, g, s):
             w_mx[e, g] = keep.tile([P, N, PACK], BF16, name=f"w_mx{e}{g}", align_bytes=64)
-            split = LAST_SPLIT if (e, g) == (E - 1, PASSES - 1) else W_SPLIT
-            interleave(nc.scalar.copy, w_mx[e, g], w_raw[e, g], 0, split)
-            if split < N:
-                interleave(nc.vector.tensor_copy, w_mx[e, g], w_raw[e, g], split, N)
+            if s:
+                interleave(nc.scalar.copy, w_mx[e, g], w_raw[e, g], 0, s)
+            if s < N:
+                interleave(nc.vector.tensor_copy, w_mx[e, g], w_raw[e, g], s, N)
 
-        def quantize_x(g, h):
-            cols = slice(h * HALF, (h + 1) * HALF)
+        def quantize_x(g, a, z):
             nc.vector.quantize_mx(
-                out=x_codes[g][:, cols].bitcast(FP8X4),
-                scales=x_scales[4 * g : P, cols],
-                in_=x_mx[g, h][:].rearrange("p n t -> p (n t)"),
+                out=x_codes[g][:, a:z].bitcast(FP8X4),
+                scales=x_scales[4 * g : P, a:z],
+                in_=x_mx[g, a][:].rearrange("p n t -> p (n t)"),
             )
 
         def quantize_w(e, g):
@@ -130,55 +134,64 @@ def tile_routed_moe_kernel(tc, xT, w, b, gate, offs, out):
                     stop=(g == PASSES - 1),
                 )
 
-        def finish(e):
-            slots = slice(e * C, (e + 1) * C)
-            y = []
-            for m in range(BLOCKS):
-                y.append(keep.tile([P, C], F32, name=f"y{e}{m}"))
-                nc.scalar.activation(y[m][:], acc[e, m][:], SILU, bias=bias[:, m, e : e + 1])
-            for m in range(BLOCKS):
-                nc.vector.tensor_tensor(
-                    windows[m][:].indirect(offsets[:, e * C // 16 : (e + 1) * C // 16]),
-                    y[m][:],
-                    gates[:, slots],
-                    MULT,
-                )
-                if e == E - 1:
-                    nc.sync.dma_start(out=out[m * P : (m + 1) * P, :], in_=windows[m][:])
+        y = {}
 
-        cast_x(0, 0)
-        cast_x(0, 1)
-        quantize_x(0, 0)
-        cast_x(1, 0)
-        quantize_x(0, 1)
-        cast_x(1, 1)
-        quantize_x(1, 0)
+        def silu(e, m):
+            y[e, m] = keep.tile([P, C], F32, name=f"y{e}{m}")
+            nc.scalar.activation(y[e, m][:], acc[e, m][:], SILU, bias=bias[:, m, e : e + 1])
+
+        def scatter(e, m):
+            nc.vector.tensor_tensor(
+                windows[m][:].indirect(offsets[:, e * C // 16 : (e + 1) * C // 16]),
+                y[e, m][:],
+                gates[:, e * C : (e + 1) * C],
+                MULT,
+            )
+
+        def store(m):
+            nc.sync.dma_start(out=out[m * P : (m + 1) * P, :], in_=windows[m][:])
+
+        cast_x(0, 0, 512, 192)
+        cast_x(0, 512, 1024, 192)
+        quantize_x(0, 0, 512)
+        cast_x(1, 0, 512, 192)
+        quantize_x(0, 512, 1024)
         gather_codes(0)
-        cast_x(2, 0)
-        quantize_x(1, 1)
-        cast_x(2, 1)
-        quantize_x(2, 0)
+        cast_x(1, 512, 1024, 192)
+        quantize_x(1, 0, 512)
+        cast_x(2, 0, 512, 320)
+        quantize_x(1, 512, 1024)
         gather_codes(1)
-        cast_w(0, 0)
-        quantize_x(2, 1)
-        cast_w(0, 1)
-        quantize_w(0, 0)
+        cast_x(2, 512, 1024, 256)
+        quantize_x(2, 0, 512)
+        cast_w(0, 0, 192)
+        quantize_x(2, 512, 1024)
+        cast_w(0, 1, 192)
         nc.vector.tensor_copy(slot_scales[:], x_scales[:].indirect(offsets[:]))
-        multiply(0, 0)
-        cast_w(0, 2)
-        quantize_w(0, 1)
+        quantize_w(0, 0)
+        cast_w(0, 2, 192)
         gather_codes(2)
+        quantize_w(0, 1)
+        multiply(0, 0)
         multiply(0, 1)
-        cast_w(1, 0)
         quantize_w(0, 2)
         multiply(0, 2)
-        cast_w(1, 1)
+        silu(0, 0)
+        silu(0, 1)
+        cast_w(1, 0, 192)
         quantize_w(1, 0)
         multiply(1, 0)
-        finish(0)
+        scatter(0, 0)
+        cast_w(1, 1, 192)
         quantize_w(1, 1)
         multiply(1, 1)
-        cast_w(1, 2)
+        cast_w(1, 2, 192)
         quantize_w(1, 2)
         multiply(1, 2)
-        finish(1)
+        silu(1, 0)
+        silu(1, 1)
+        scatter(0, 1)
+        scatter(1, 0)
+        store(0)
+        scatter(1, 1)
+        store(1)

@@ -53,12 +53,12 @@ def tile_routed_moe_kernel(tc, xT, w, b, gate, offs, out):
         load_x(1, 0, 1024)
         load_x(2, 0, 512)
         load_x(2, 512, 1024)
-        nc.sync.dma_start(out=gates[:], in_=gate[0:P, :])
         load_w(0, 0)
         load_w(0, 1)
         load_w(0, 2)
         load_w(1, 0)
         load_w(1, 1)
+        nc.sync.dma_start(out=gates[:], in_=gate[0:P, :])
         load_w(1, 2)
 
         warm = keep.tile([P, 1], F32, name="warm")
@@ -91,7 +91,10 @@ def tile_routed_moe_kernel(tc, xT, w, b, gate, offs, out):
                 interleave(nc.vector.tensor_copy, x_mx[g, a], x_raw[g, a], s, z - a)
 
         def cast_w(e, g, s):
-            w_mx[e, g] = keep.tile([P, N, PACK], BF16, name=f"w_mx{e}{g}", align_bytes=64)
+            if (e, g) == (E - 1, PASSES - 1):
+                w_mx[e, g] = keep.tile([P, N, PACK], BF16, name=f"w_mx{e}{g}", tag="turn", align_bytes=64)
+            else:
+                w_mx[e, g] = keep.tile([P, N, PACK], BF16, name=f"w_mx{e}{g}", align_bytes=64)
             if s:
                 interleave(nc.scalar.copy, w_mx[e, g], w_raw[e, g], 0, s)
             if s < N:
@@ -137,7 +140,10 @@ def tile_routed_moe_kernel(tc, xT, w, b, gate, offs, out):
         y = {}
 
         def silu(e, m):
-            y[e, m] = keep.tile([P, C], F32, name=f"y{e}{m}")
+            if (e, m) == (0, 1):
+                y[e, m] = keep.tile([P, C], F32, name=f"y{e}{m}", tag="turn", align_bytes=64)
+            else:
+                y[e, m] = keep.tile([P, C], F32, name=f"y{e}{m}")
             nc.scalar.activation(y[e, m][:], acc[e, m][:], SILU, bias=bias[:, m, e : e + 1])
 
         def scatter(e, m):
@@ -151,45 +157,45 @@ def tile_routed_moe_kernel(tc, xT, w, b, gate, offs, out):
         def store(m):
             nc.sync.dma_start(out=out[m * P : (m + 1) * P, :], in_=windows[m][:])
 
-        cast_x(0, 0, 512, 192)
-        cast_x(0, 512, 1024, 192)
+        cast_x(0, 0, 512, 0)
+        cast_x(0, 512, 1024, 320)
         quantize_x(0, 0, 512)
-        cast_x(1, 0, 512, 192)
+        cast_x(1, 0, 512, 256)
         quantize_x(0, 512, 1024)
         gather_codes(0)
-        cast_x(1, 512, 1024, 192)
+        cast_x(1, 512, 1024, 128)
         quantize_x(1, 0, 512)
-        cast_x(2, 0, 512, 320)
+        cast_x(2, 0, 512, 384)
         quantize_x(1, 512, 1024)
         gather_codes(1)
         cast_x(2, 512, 1024, 256)
         quantize_x(2, 0, 512)
-        cast_w(0, 0, 192)
+        cast_w(0, 0, 128)
         quantize_x(2, 512, 1024)
-        cast_w(0, 1, 192)
+        cast_w(0, 1, 256)
         nc.vector.tensor_copy(slot_scales[:], x_scales[:].indirect(offsets[:]))
-        quantize_w(0, 0)
-        cast_w(0, 2, 192)
         gather_codes(2)
-        quantize_w(0, 1)
+        quantize_w(0, 0)
         multiply(0, 0)
+        cast_w(0, 2, 256)
+        quantize_w(0, 1)
         multiply(0, 1)
         quantize_w(0, 2)
         multiply(0, 2)
         silu(0, 0)
-        silu(0, 1)
-        cast_w(1, 0, 192)
+        cast_w(1, 0, 256)
         quantize_w(1, 0)
         multiply(1, 0)
-        scatter(0, 0)
-        cast_w(1, 1, 192)
+        cast_w(1, 1, 64)
         quantize_w(1, 1)
         multiply(1, 1)
-        cast_w(1, 2, 192)
+        scatter(0, 0)
+        cast_w(1, 2, 256)
         quantize_w(1, 2)
         multiply(1, 2)
         silu(1, 0)
         silu(1, 1)
+        silu(0, 1)
         scatter(0, 1)
         scatter(1, 0)
         store(0)

@@ -34,6 +34,10 @@ def tile_routed_moe_kernel(tc, xT, w, b, gate, offs, out):
         offsets = keep.tile([P, SLOTS // 16], U16, name="offsets")
         bias = keep.tile([P, BLOCKS, E], F32, name="bias")
         gates = keep.tile([P, SLOTS], F32, name="gates")
+        gate_row = keep.tile([P, SLOTS], F32, name="gate_row")
+        nc.vector.memset(gate_row[:], 0.0)
+        ones = keep.tile([P, P], F32, name="ones")
+        nc.vector.memset(ones[:], 1.0)
         x_raw, w_raw = {}, {}
 
         def load_x(g, a, z):
@@ -43,12 +47,16 @@ def tile_routed_moe_kernel(tc, xT, w, b, gate, offs, out):
                 x_raw[g, token] = raw[:, :, token - a : min(z, token + PIECE) - a]
 
         def load_w(e, g):
-            raw = keep.tile([P, PACK, N], F32, name=f"w_raw{e}{g}", align_bytes=64)
+            if (e, g) == (E - 1, PASSES - 1):
+                raw = keep.tile([P, PACK, N], F32, name=f"w_raw{e}{g}", tag="turn", align_bytes=64)
+            else:
+                raw = keep.tile([P, PACK, N], F32, name=f"w_raw{e}{g}", align_bytes=64)
             nc.sync.dma_start(out=raw[:], in_=w_rows[e, g])
             w_raw[e, g] = raw[:]
 
         load_x(0, 0, 1024)
         nc.sync.dma_start(offsets[:], offs)
+        nc.sync.dma_start(out=gate_row[0:1, :], in_=gate[0:1, :])
         nc.scalar.dma_start(out=bias[:], in_=b.rearrange("(m p) e -> p m e", p=P))
         load_x(1, 0, 1024)
         load_x(2, 0, 512)
@@ -58,7 +66,6 @@ def tile_routed_moe_kernel(tc, xT, w, b, gate, offs, out):
         load_w(0, 2)
         load_w(1, 0)
         load_w(1, 1)
-        nc.sync.dma_start(out=gates[:], in_=gate[0:P, :])
         load_w(1, 2)
 
         warm = keep.tile([P, 1], F32, name="warm")
@@ -91,10 +98,7 @@ def tile_routed_moe_kernel(tc, xT, w, b, gate, offs, out):
                 interleave(nc.vector.tensor_copy, x_mx[g, a], x_raw[g, a], s, z - a)
 
         def cast_w(e, g, s):
-            if (e, g) == (E - 1, PASSES - 1):
-                w_mx[e, g] = keep.tile([P, N, PACK], BF16, name=f"w_mx{e}{g}", tag="turn", align_bytes=64)
-            else:
-                w_mx[e, g] = keep.tile([P, N, PACK], BF16, name=f"w_mx{e}{g}", align_bytes=64)
+            w_mx[e, g] = keep.tile([P, N, PACK], BF16, name=f"w_mx{e}{g}", align_bytes=64)
             if s:
                 interleave(nc.scalar.copy, w_mx[e, g], w_raw[e, g], 0, s)
             if s < N:
@@ -170,6 +174,9 @@ def tile_routed_moe_kernel(tc, xT, w, b, gate, offs, out):
         gather_codes(1)
         cast_x(2, 512, 1024, 256)
         quantize_x(2, 0, 512)
+        gate_sums = psum.tile([P, SLOTS], F32, name="gate_sums")
+        nc.tensor.matmul(gate_sums[:], ones[:], gate_row[:], start=True, stop=True)
+        nc.scalar.copy(gates[:], gate_sums[:])
         cast_w(0, 0, 128)
         quantize_x(2, 512, 1024)
         cast_w(0, 1, 256)
@@ -191,11 +198,11 @@ def tile_routed_moe_kernel(tc, xT, w, b, gate, offs, out):
         multiply(1, 1)
         scatter(0, 0)
         cast_w(1, 2, 256)
+        silu(0, 1)
         quantize_w(1, 2)
         multiply(1, 2)
         silu(1, 0)
         silu(1, 1)
-        silu(0, 1)
         scatter(0, 1)
         scatter(1, 0)
         store(0)

from contextlib import ExitStack

import concourse.mybir as mybir

K, T, E, C, N = 1536, 1024, 2, 256, 256
FLOPS = 2 * K * N * E * C

F32 = mybir.dt.float32
BF16 = mybir.dt.bfloat16
U32 = mybir.dt.uint32
U16 = mybir.dt.uint16
U8 = mybir.dt.uint8
FP8X4 = mybir.dt.float8_e4m3fn_x4
SILU = mybir.ActivationFunctionType.Silu
MULT = mybir.AluOpType.mult

P = 128
PACK = 4
PASSES = K // (P * PACK)
BLOCKS = N // P
SLOTS = E * C
PIECE = 512


def tile_routed_moe_kernel(tc, xT, w, b, gate, offs, out):
    nc = tc.nc
    x_rows = xT.rearrange("(g p t) n -> g p t n", p=P, t=PACK)
    w_rows = w.rearrange("e (g p t) n -> e g p t n", p=P, t=PACK)

    with ExitStack() as ctx:
        keep = ctx.enter_context(tc.tile_pool(name="keep", bufs=1))
        psum = ctx.enter_context(tc.psum_pool(name="psum", bufs=1))

        offsets = keep.tile([P, SLOTS // 16], U16, name="offsets")
        bias = keep.tile([P, BLOCKS, E], F32, name="bias")
        gates = keep.tile([P, SLOTS], F32, name="gates")
        gate_row = keep.tile([P, SLOTS], F32, name="gate_row")
        nc.vector.memset(gate_row[:], 0.0)
        ones = keep.tile([P, P], F32, name="ones")
        nc.vector.memset(ones[:], 1.0)
        x_raw, w_raw = {}, {}

        def load_x(g, a, z):
            raw = keep.tile([P, PACK, z - a], F32, name=f"x_raw{g}_{a}", align_bytes=64)
            nc.sync.dma_start(out=raw[:], in_=x_rows[g, :, :, a:z])
            for token in range(a, z, PIECE):
                x_raw[g, token] = raw[:, :, token - a : min(z, token + PIECE) - a]

        def load_w(e, g):
            if (e, g) == (E - 1, PASSES - 1):
                raw = keep.tile([P, PACK, N], F32, name=f"w_raw{e}{g}", tag="turn", align_bytes=64)
            else:
                raw = keep.tile([P, PACK, N], F32, name=f"w_raw{e}{g}", align_bytes=64)
            nc.sync.dma_start(out=raw[:], in_=w_rows[e, g])
            w_raw[e, g] = raw[:]

        load_x(0, 0, 1024)
        nc.sync.dma_start(offsets[:], offs)
        nc.sync.dma_start(out=gate_row[0:1, :], in_=gate[0:1, :])
        nc.scalar.dma_start(out=bias[:], in_=b.rearrange("(m p) e -> p m e", p=P))
        load_x(1, 0, 1024)
        load_x(2, 0, 512)
        load_x(2, 512, 1024)
        load_w(0, 0)
        load_w(0, 1)
        load_w(0, 2)
        load_w(1, 0)
        load_w(1, 1)
        load_w(1, 2)

        warm = keep.tile([P, 1], F32, name="warm")
        nc.vector.memset(warm[:], 0.0)
        nc.scalar.activation(warm[:], warm[:], SILU)

        x_scales = keep.tile([P, T], U8, name="x_scales", align_bytes=64)
        nc.gpsimd.memset(x_scales[:], 0)
        windows = []
        for m in range(BLOCKS):
            windows.append(keep.tile([P, T], F32, name=f"window{m}"))
            nc.gpsimd.memset(windows[m][:], 0.0)

        x_codes = [keep.tile([P, T], U32, name=f"x_codes{g}", align_bytes=64) for g in range(PASSES)]
        slot_codes = [keep.tile([P, SLOTS], U32, name=f"slot_codes{g}", align_bytes=64) for g in range(PASSES)]
        slot_scales = keep.tile([P, SLOTS], U8, name="slot_scales", align_bytes=64)
        x_mx, w_mx, w_codes, w_scales = {}, {}, {}, {}

        def interleave(copy, dst, raw, a, z):
            copy(
                dst[:, a:z, :].rearrange("p (c i) t -> p c t i", i=4),
                raw[:, :, a:z].rearrange("p t (c i) -> p c t i", i=4),
            )

        def cast_x(g, a, z, s):
            x_mx[g, a] = keep.tile([P, z - a, PACK], BF16, name=f"x_mx{g}_{a}", align_bytes=64)
            if s:
                interleave(nc.scalar.copy, x_mx[g, a], x_raw[g, a], 0, s)
            if s < z - a:
                interleave(nc.vector.tensor_copy, x_mx[g, a], x_raw[g, a], s, z - a)

        def cast_w(e, g, s):
            w_mx[e, g] = keep.tile([P, N, PACK], BF16, name=f"w_mx{e}{g}", align_bytes=64)
            if s:
                interleave(nc.scalar.copy, w_mx[e, g], w_raw[e, g], 0, s)
            if s < N:
                interleave(nc.vector.tensor_copy, w_mx[e, g], w_raw[e, g], s, N)

        def quantize_x(g, a, z):
            nc.vector.quantize_mx(
                out=x_codes[g][:, a:z].bitcast(FP8X4),
                scales=x_scales[4 * g : P, a:z],
                in_=x_mx[g, a][:].rearrange("p n t -> p (n t)"),
            )

        def quantize_w(e, g):
            w_codes[e, g] = keep.tile([P, N], U32, name=f"w_codes{e}{g}", align_bytes=64)
            w_scales[e, g] = keep.tile([P, N], U8, name=f"w_scales{e}{g}", align_bytes=64)
            nc.vector.quantize_mx(
                out=w_codes[e, g][:].bitcast(FP8X4),
                scales=w_scales[e, g][:],
                in_=w_mx[e, g][:].rearrange("p n t -> p (n t)"),
            )

        def gather_codes(g):
            nc.vector.tensor_copy(slot_codes[g][:], x_codes[g][:].indirect(offsets[:]))

        acc = {}

        def multiply(e, g):
            slots = slice(e * C, (e + 1) * C)
            for m in range(BLOCKS):
                if g == 0:
                    acc[e, m] = psum.tile([P, C], F32, name=f"acc{e}{m}")
                feats = slice(m * P, (m + 1) * P)
                nc.tensor.matmul_mx(
                    out=acc[e, m][:],
                    lhsT=w_codes[e, g][:, feats].bitcast(FP8X4),
                    lhsT_scale=w_scales[e, g][:, feats],
                    rhs=slot_codes[g][:, slots].bitcast(FP8X4),
                    rhs_scale=slot_scales[4 * g : P, slots],
                    start=(g == 0),
                    stop=(g == PASSES - 1),
                )

        y = {}

        def silu(e, m):
            if (e, m) == (0, 1):
                y[e, m] = keep.tile([P, C], F32, name=f"y{e}{m}", tag="turn", align_bytes=64)
            else:
                y[e, m] = keep.tile([P, C], F32, name=f"y{e}{m}")
            nc.scalar.activation(y[e, m][:], acc[e, m][:], SILU, bias=bias[:, m, e : e + 1])

        def scatter(e, m):
            nc.vector.tensor_tensor(
                windows[m][:].indirect(offsets[:, e * C // 16 : (e + 1) * C // 16]),
                y[e, m][:],
                gates[:, e * C : (e + 1) * C],
                MULT,
            )

        def store(m):
            nc.sync.dma_start(out=out[m * P : (m + 1) * P, :], in_=windows[m][:])

        cast_x(0, 0, 512, 0)
        cast_x(0, 512, 1024, 320)
        quantize_x(0, 0, 512)
        cast_x(1, 0, 512, 256)
        quantize_x(0, 512, 1024)
        gather_codes(0)
        cast_x(1, 512, 1024, 128)
        quantize_x(1, 0, 512)
        cast_x(2, 0, 512, 384)
        quantize_x(1, 512, 1024)
        gather_codes(1)
        cast_x(2, 512, 1024, 256)
        quantize_x(2, 0, 512)
        gate_sums = psum.tile([P, SLOTS], F32, name="gate_sums")
        nc.tensor.matmul(gate_sums[:], ones[:], gate_row[:], start=True, stop=True)
        nc.scalar.copy(gates[:], gate_sums[:])
        cast_w(0, 0, 128)
        quantize_x(2, 512, 1024)
        cast_w(0, 1, 256)
        nc.vector.tensor_copy(slot_scales[:], x_scales[:].indirect(offsets[:]))
        gather_codes(2)
        quantize_w(0, 0)
        multiply(0, 0)
        cast_w(0, 2, 256)
        quantize_w(0, 1)
        multiply(0, 1)
        quantize_w(0, 2)
        multiply(0, 2)
        silu(0, 0)
        cast_w(1, 0, 256)
        quantize_w(1, 0)
        multiply(1, 0)
        cast_w(1, 1, 64)
        quantize_w(1, 1)
        multiply(1, 1)
        scatter(0, 0)
        cast_w(1, 2, 256)
        silu(0, 1)
        quantize_w(1, 2)
        multiply(1, 2)
        silu(1, 0)
        silu(1, 1)
        scatter(0, 1)
        scatter(1, 0)
        store(0)
        scatter(1, 1)
        store(1)
